import numpy as np, ml_dtypes
CORES = [83,85,87,115,117,119]
N = 6
import mx_ref
NC, G = 256, 4
C = np.float32(0.023)
CNT = [[24,40,0,40,40,112],[24,0,40,96,56,40],[40,0,80,32,64,40],[56,120,80,0,0,0],[40,0,32,64,56,64],[72,96,24,24,40,0]]
OFF = [[sum(c[:e]) for e in range(N + 1)] for c in CNT]
BF = ml_dtypes.bfloat16
def cut(t, i, w=512):
    return t[:, w * i:w * i + w]
def tile(rs):
    return np.stack(rs, axis=2).reshape(128, -1).astype(BF)
def layer(w, X):
    out = []
    for i in range(G):
        for t in range(len(X)):
            p = mx_ref.matmul(mx_ref.quantize(cut(w, len(X) * i + t)), X[t])
            z = p if t == 0 else z + p
        out.append(z)
    return out
def act(Z):
    return [np.maximum(z, 0) * C for z in Z]
def setup_inputs(rng):
    def f(*shape):
        return mx_ref.flush((rng.standard_normal(shape, dtype=np.float32) * np.exp2(rng.integers(-2, 3, shape[:-1] + (1,)))).astype(BF))
    return {"x": f(N, 128, 4 * NC), "w1": f(N, 128, G * 512), "w2": f(N, 128, 512), "s1": f(N, 128, G * 512), "s2": f(N, 128, 512)}
def setup_inputs_blocks(rng):
    d = setup_inputs(rng)
    for k in ("x", "w1", "w2", "s1", "s2"): d[k] = mx_ref.spread(d[k], rng, 4)
    return d
def setup_inputs_wide(rng):
    d = setup_inputs(rng)
    for k in ("x", "w1", "w2", "s1", "s2"): d[k] = mx_ref.flush((d[k].astype(np.float32) * np.exp2(rng.integers(-8, 9, (N, 1, 1))).astype(np.float32)).astype(BF))
    return d
def setup_inputs_zeros(rng):
    d = setup_inputs(rng); v = d["x"].reshape(N, 128, -1, 4).copy()
    v[np.broadcast_to((rng.random((N, 1, v.shape[2], 1)) < 0.33), v.shape)] = 0
    d["x"] = v.reshape(d["x"].shape)
    return d
def reference(x, w1, w2, s1, s2):
    y = np.zeros((N, 128, NC), np.float32)
    for j in range(N):
        y[j] = mx_ref.matmul(mx_ref.quantize(s2[j]), mx_ref.quantize(tile(act(layer(s1[j], [mx_ref.quantize(x[j])])))))
    for e in range(N):
        t = np.concatenate([x[j][:, 4 * OFF[j][e]:4 * OFF[j][e + 1]] for j in range(N)], axis=1)
        p = mx_ref.matmul(mx_ref.quantize(w2[e]), mx_ref.quantize(tile(act(layer(w1[e], [mx_ref.quantize(t)])))))
        c = 0
        for j in range(N):
            a, b = OFF[j][e], OFF[j][e + 1]
            y[j][:, a:b] = y[j][:, a:b] + p[:, c:c + b - a]; c += b - a
    return {"y": y}

@@ -1,0 +1,308 @@
+from concourse.bass import DstId, RemoteDMATransfer
+from concourse.mybir import dt, AluOpType, ActivationFunctionType
+
+C = 0.023
+NC = 256
+SEND = [
+    [(40, {3: 1, 4: 1, 1: 1}), (112, {5: 1})],
+    [(40, {5: 1, 3: 1, 0: 1, 2: 1}), (56, {4: 1, 3: 1})],
+    [(40, {3: 1, 5: 1, 0: 1}), (64, {4: 1})],
+    [(60, {0: 1, 1: 2}), (80, {2: 1})],
+    [(40, {0: 1, 2: 1}), (64, {3: 1, 5: 1})],
+    [(72, {0: 1, 1: 1}), (24, {1: 1, 2: 1, 3: 1, 4: 2})],
+]
+RET = [
+    [(72, {5: 1}, 0), (56, {3: 1}, 0), (40, {4: 1, 2: 1}, 1), (24, {1: 1}, 1)],
+    [(120, {3: 1}, 0), (96, {5: 1}, 1), (40, {0: 1}, 1)],
+    [(40, {3: 2, 1: 1}, 0), (32, {4: 1}, 1), (24, {5: 1}, 1)],
+    [(96, {1: 1}, 0), (32, {2: 1}, 0), (40, {0: 1, 4: 1}, 1), (24, {4: 1, 5: 1}, 1)],
+    [(64, {2: 1}, 0), (56, {1: 1}, 0), (40, {0: 1, 5: 1}, 1)],
+    [(112, {0: 1}, 0), (40, {1: 1, 2: 1}, 1), (64, {4: 1}, 1)],
+]
+ORDER = [[5, 3, 4, 2, 1], [3, 5, 0], [3, 1, 4, 5], [1, 2, 0, 4, 5], [2, 1, 0, 5], [0, 1, 2, 4]]
+LMAX = 272
+
+SCRATCH = {
+    "xt": ("sbuf", [128, 4 * NC], "bfloat16"),
+    "w1t": ("sbuf", [128, 2048], "bfloat16"),
+    "w2t": ("sbuf", [128, 512], "bfloat16"),
+    "s1t": ("sbuf", [128, 2048], "bfloat16"),
+    "s2t": ("sbuf", [128, 512], "bfloat16"),
+    "xq": ("sbuf", [128, LMAX + NC], "float8_e4m3fn_x4"),
+    "xs": ("sbuf", [128, LMAX + NC], "uint8"),
+    "w1q": ("sbuf", [128, 512], "float8_e4m3fn_x4"),
+    "w1s": ("sbuf", [128, 512], "uint8"),
+    "w2q": ("sbuf", [128, 128], "float8_e4m3fn_x4"),
+    "w2s": ("sbuf", [128, 128], "uint8"),
+    "s1q": ("sbuf", [128, 512], "float8_e4m3fn_x4"),
+    "s1s": ("sbuf", [128, 512], "uint8"),
+    "s2q": ("sbuf", [128, 128], "float8_e4m3fn_x4"),
+    "s2s": ("sbuf", [128, 128], "uint8"),
+    "ha": ("sbuf", [128, 4 * NC], "bfloat16"),
+    "hb": ("sbuf", [128, 4 * NC], "bfloat16"),
+    "haq": ("sbuf", [128, NC], "float8_e4m3fn_x4"),
+    "has": ("sbuf", [128, NC], "uint8"),
+    "hbq": ("sbuf", [128, NC], "float8_e4m3fn_x4"),
+    "hbs": ("sbuf", [128, NC], "uint8"),
+    "kt": ("sbuf", [128, 4 * NC], "bfloat16"),
+    "kq": ("sbuf", [128, NC], "float8_e4m3fn_x4"),
+    "ks": ("sbuf", [128, NC], "uint8"),
+    "p": ("sbuf", [128, LMAX + NC], "float32"),
+    "land": ("sbuf", [128, NC], "float32"),
+    "yt": ("sbuf", [128, NC], "float32"),
+    "ps": ("psum", [128, 512 * 8], "float32"),
+}
+SEMAPHORES = (["ldx", "ldw1", "ldw2", "lds1", "lds2", "issued", "qx", "qw1", "qw2", "qs1", "qs2", "xin", "sent"]
+              + ["z%d" % i for i in range(8)] + ["y%d" % i for i in range(4)]
+              + ["ha4", "hb4", "k4", "qha", "qhb", "qk", "ppa", "ppb", "cpa", "cpb", "cpl", "u",
+                 "reton", "retoff", "addon", "addoff", "ston", "stoff"])
+
+
+def bits(mask):
+    return [i for i in range(16) if mask >> i & 1]
+
+
+def engines(src, dsts, topo):
+    far = [d for d in dsts if topo.chip(d) != topo.chip(src)]
+    near = [d for d in dsts if topo.chip(d) == topo.chip(src)]
+    out, taken = {}, 0
+    for group in (far, near):
+        if not group:
+            continue
+        free = bits(topo.mask(src, group[0]) & ~taken)
+        base = 1
+        while base * 2 * len(group) <= len(free):
+            base *= 2
+        size = [base] * len(group)
+        for i in range(len(group)):
+            if sum(size) + size[i] <= len(free):
+                size[i] *= 2
+        at = 0
+        for i, d in enumerate(group):
+            m = sum(1 << b for b in free[at:at + size[i]])
+            at += size[i]
+            out.setdefault(d, []).append((m, size[i]))
+        taken |= topo.mask(src, group[0])
+    return out
+
+
+def make_plan(CNT, cores, topo):
+    N = len(cores)
+    off = [[sum(c[:e]) for e in range(N + 1)] for c in CNT]
+    base = [off[j][j] if CNT[j][j] else 0 for j in range(N)]
+    rot = [[(off[j][e] - base[j]) % NC for e in range(N)] for j in range(N)]
+    total = {}
+    for j in range(N):
+        for w, ds in SEND[j]:
+            for e, k in ds.items():
+                total[j, e] = total.get((j, e), 0) + w * k
+    lw = [sum(total[j, e] for j in ORDER[e]) for e in range(N)]
+    L = [-(-w // 16) * 16 for w in lw]
+    first = [L[e] - lw[e] for e in range(N)]
+    n = [lw[e] + CNT[e][e] for e in range(N)]
+    mid = [n[e] - 128 for e in range(N)]
+    land, real, win = {}, {}, {}
+    for e in range(N):
+        p = first[e]
+        for j in ORDER[e]:
+            win[j, e] = min(rot[j][e], NC - total[j, e])
+            land[j, e] = p
+            real[j, e] = p - first[e] + rot[j][e] - win[j, e]
+            p += total[j, e]
+    sends, xin = [], [0] * N
+    for j in range(N):
+        done, calls = {}, []
+        for w, ds in SEND[j]:
+            lst = [e for e, k in ds.items() for _ in range(k)]
+            em = engines(cores[j], [cores[e] for e in lst], topo)
+            tr = []
+            for e in lst:
+                m, k = em[cores[e]].pop(0)
+                d = done.get(e, 0)
+                tr.append((e, win[j, e] + d, land[j, e] + d, m, k))
+                done[e] = d + w
+                xin[e] += 2 * k
+            calls.append((w, tr))
+        sends.append(calls)
+    rets = []
+    ron, roff = [0] * N, [0] * N
+    for e in range(N):
+        done, calls = {}, []
+        for w, ds, part in RET[e]:
+            lst = [j for j, k in ds.items() for _ in range(k)]
+            em = engines(cores[e], [cores[j] for j in lst], topo)
+            tr = []
+            for j in lst:
+                m, k = em[cores[j]].pop(0)
+                d = done.get(j, 0)
+                p = real[j, e] + d
+                assert part or p + w <= mid[e], (e, j, p, w, mid[e])
+                tr.append((j, p, rot[j][e] + d, m, k))
+                done[j] = d + w
+                if topo.chip(cores[e]) == topo.chip(cores[j]):
+                    ron[j] += k
+                else:
+                    roff[j] += k
+            calls.append((w, tr, part))
+        for j in range(N):
+            assert done.get(j, 0) == (CNT[j][e] if j != e else 0), (e, j)
+        rets.append(calls)
+    ranges = []
+    for j in range(N):
+        rs = []
+        for e in sorted(range(N), key=lambda e: rot[j][e]):
+            if not CNT[j][e]:
+                continue
+            far = topo.chip(cores[e]) != topo.chip(cores[j])
+            a = rot[j][e]
+            if rs and rs[-1][2] == far and off[j][e] != 0:
+                rs[-1][1] = a + CNT[j][e]
+            else:
+                rs.append([a, a + CNT[j][e], far])
+        ranges.append(rs)
+    return dict(L=L, first=first, n=n, mid=mid, base=base, sends=sends, xin=xin, rets=rets, ron=ron, roff=roff, ranges=ranges)
+
+
+def rank_program(g, core, T, topo):
+    rank = T.rank_of(core)
+    if rank is None:
+        return
+    CNT = T.tables["CNT"]
+    cores = T.cores
+    P = make_plan(CNT, cores, topo)
+    S = T.sem
+    L, first, n, mid, base = P["L"][rank], P["first"][rank], P["n"][rank], P["mid"][rank], P["base"][rank]
+    own = CNT[rank][rank]
+    U8 = dt.uint8
+    sizes = (mid, n - mid)
+
+    def bank(k, w):
+        return T.ps[:, 512 * k:512 * k + w]
+
+    def dst(c):
+        rid, pid, _ = topo.addr(c)
+        return DstId(rid=rid, pnc=pid)
+
+    sent = [0]
+
+    def fused(trs, sem):
+        g.remote_dma_fused([RemoteDMATransfer(dst_ids=[dst(c)], dma_engine_mask=m, remote_sem=sem[i], srcs=[s], dsts=[d])
+                            for i, (c, d, s, m, k) in enumerate(trs)], local_sem=S.sent)
+        sent[0] += sum(t[4] for t in trs)
+
+    cut = NC - base
+    g.sync.dma_start(T.xt[:, 0:4 * cut], T.x[:, 4 * base:4 * NC]).then_inc(S.ldx, 16)
+    if base:
+        g.scalar.dma_start(T.xt[:, 4 * cut:4 * NC], T.x[:, 0:4 * base]).then_inc(S.ldx, 16)
+    g.sync.dma_start(T.w1t[:], T.w1[:]).then_inc(S.ldw1, 16)
+    g.sync.dma_start(T.w2t[:], T.w2[:]).then_inc(S.ldw2, 16)
+    g.sync.wait_ge(S.issued, 1)
+    g.sync.dma_start(T.s1t[:], T.s1[:]).then_inc(S.lds1, 16)
+    g.sync.dma_start(T.s2t[:], T.s2[:]).then_inc(S.lds2, 16)
+
+    g.wait_ge(S.qx, 1)
+    for w, tr in P["sends"][rank]:
+        fused([(cores[e], T.xq[:, d:d + w].bitcast(U8), T.xq[:, L + s:L + s + w].bitcast(U8), m, k) for e, s, d, m, k in tr],
+              [S.xin] * len(tr))
+    for w, tr in P["sends"][rank]:
+        fused([(cores[e], T.xs[:, d:d + w], T.xs[:, L + s:L + s + w], m, k) for e, s, d, m, k in tr],
+              [S.xin] * len(tr))
+    g.sem_inc(S.issued, 1)
+    have = 0
+    for w, tr, part in P["rets"][rank]:
+        if have <= part:
+            for sem in (S.cpa, S.cpb)[have:part + 1]:
+                g.wait_ge(sem, 1)
+            have = part + 1
+        fused([(cores[j], T.land[:, d:d + w], T.p[:, s:s + w], m, k) for j, s, d, m, k in tr],
+              [S.reton if topo.chip(cores[j]) == topo.chip(core) else S.retoff for j, s, d, m, k in tr])
+    g.wait_ge(S.sent, sent[0])
+
+    t = g.tensor
+    t.wait_ge(S.qw1, 1)
+    t.wait_ge(S.qx, 1)
+    t.wait_ge(S.xin, P["xin"][rank])
+    for part in (0, 1):
+        a = first + (mid if part else 0)
+        b = a + sizes[part]
+        for i in range(4):
+            t.matmul_mx(bank(4 * part + i, sizes[part]), T.w1q[:, 128 * i:128 * i + 128], T.w1s[:, 128 * i:128 * i + 128],
+                        T.xq[:, a:b], T.xs[:, a:b], True, True).then_inc(S["z%d" % (4 * part + i)], 1)
+    t.wait_ge(S.qw2, 1)
+    for part in (0, 1):
+        t.wait_ge(S["qhb"] if part else S["qha"], 1)
+        q, s = (T.hbq, T.hbs) if part else (T.haq, T.has)
+        t.matmul_mx(bank(4 * part, sizes[part]), T.w2q[:], T.w2s[:], q[:, 0:sizes[part]], s[:, 0:sizes[part]],
+                    True, True).then_inc(S["ppb"] if part else S["ppa"], 1)
+    YB = (1, 2, 3, 5)
+    t.wait_ge(S.qs1, 1)
+    for i in range(4):
+        t.matmul_mx(bank(YB[i], NC), T.s1q[:, 128 * i:128 * i + 128], T.s1s[:, 128 * i:128 * i + 128],
+                    T.xq[:, L:L + NC], T.xs[:, L:L + NC], True, True).then_inc(S["y%d" % i], 1)
+    t.wait_ge(S.qs2, 1)
+    t.wait_ge(S.qk, 1)
+    t.matmul_mx(bank(6, NC), T.s2q[:], T.s2s[:], T.kq[:], T.ks[:], True, True).then_inc(S.u, 1)
+
+    v, sc = g.vector, g.scalar
+
+    def step_v(out, in_, sem):
+        v.tensor_scalar(out, in_, 0.0, C, AluOpType.max, AluOpType.mult).then_inc(sem, 1)
+
+    def step_s(out, in_, sem):
+        sc.activation(out, in_, ActivationFunctionType.Relu, scale=C).then_inc(sem, 1)
+
+    v.wait_ge(S.ldx, 32 if base else 16)
+    v.quantize_mx(T.xq[:, L:L + NC], T.xs[:, L:L + NC], T.xt[:]).then_inc(S.qx, 1)
+    v.wait_ge(S.ldw1, 16)
+    v.quantize_mx(T.w1q[:], T.w1s[:], T.w1t[:]).then_inc(S.qw1, 1)
+    v.wait_ge(S.ldw2, 16)
+    v.quantize_mx(T.w2q[:], T.w2s[:], T.w2t[:]).then_inc(S.qw2, 1)
+    for part in (0, 1):
+        w = sizes[part]
+        h, q, s = (T.hb, T.hbq, T.hbs) if part else (T.ha, T.haq, T.has)
+        done = S["hb4"] if part else S["ha4"]
+        for i in (0, 2):
+            sc.wait_ge(S["z%d" % (4 * part + i)], 1)
+            step_s(h[:, i:4 * w:4], bank(4 * part + i, w), done)
+        for i in (1, 3):
+            v.wait_ge(S["z%d" % (4 * part + i)], 1)
+            step_v(h[:, i:4 * w:4], bank(4 * part + i, w), done)
+        v.wait_ge(done, 4)
+        v.quantize_mx(q[:, 0:w], s[:, 0:w], h[:, 0:4 * w]).then_inc(S["qhb"] if part else S["qha"], 1)
+    sc.wait_ge(S.ppa, 1)
+    sc.activation(T.p[:, 0:mid], bank(0, mid), ActivationFunctionType.Copy).then_inc(S.cpa, 1)
+    v.wait_ge(S.ppb, 1)
+    wb = sizes[1]
+    v.tensor_copy(T.p[:, mid:n - own], bank(4, wb - own)).then_inc(S.cpb, 1)
+    if own:
+        v.tensor_copy(T.land[:, 0:own], T.ps[:, 512 * 4 + wb - own:512 * 4 + wb]).then_inc(S.cpl, 1)
+    v.wait_ge(S.lds1, 16)
+    v.quantize_mx(T.s1q[:], T.s1s[:], T.s1t[:]).then_inc(S.qs1, 1)
+    v.wait_ge(S.lds2, 16)
+    v.quantize_mx(T.s2q[:], T.s2s[:], T.s2t[:]).then_inc(S.qs2, 1)
+    for i in (0, 2):
+        sc.wait_ge(S["y%d" % i], 1)
+        step_s(T.kt[:, i:4 * NC:4], bank(YB[i], NC), S.k4)
+    for i in (1, 3):
+        v.wait_ge(S["y%d" % i], 1)
+        step_v(T.kt[:, i:4 * NC:4], bank(YB[i], NC), S.k4)
+    v.wait_ge(S.k4, 4)
+    v.quantize_mx(T.kq[:], T.ks[:], T.kt[:]).then_inc(S.qk, 1)
+
+    v.wait_ge(S.u, 1)
+    if own:
+        v.wait_ge(S.cpl, 1)
+    for far, ret, add, st, q in ((False, "reton", "addon", "ston", sc), (True, "retoff", "addoff", "stoff", g.sync)):
+        rs = [r for r in P["ranges"][rank] if r[2] == far]
+        if not rs:
+            continue
+        count = P["roff" if far else "ron"][rank]
+        if count:
+            v.wait_ge(S[ret], count)
+        for a, b, _ in rs:
+            v.tensor_tensor(T.yt[:, a:b], T.ps[:, 512 * 6 + a:512 * 6 + b], T.land[:, a:b], AluOpType.add).then_inc(S[add], 1)
+        q.wait_ge(S[add], len(rs))
+        for a, b, _ in rs:
+            c = (a + base) % NC
+            q.dma_start(T.y[:, c:c + b - a], T.yt[:, a:b]).then_inc(S[st], 16)
+        q.wait_ge(S[st], 16 * len(rs))

@@ -3,26 +3,29 @@ from concourse.mybir import dt, AluOpType, ActivationFunctionType
 
 C = 0.023
 NC = 256
+LEAST = 128
+BASE = [0, 160, 0, 0, 0, 0]
 SEND = [
-    [(40, {3: 1, 4: 1, 1: 1}), (112, {5: 1})],
-    [(40, {5: 1, 3: 1, 0: 1, 2: 1}), (56, {4: 1, 3: 1})],
-    [(40, {3: 1, 5: 1, 0: 1}), (64, {4: 1})],
-    [(60, {0: 1, 1: 2}), (80, {2: 1})],
-    [(40, {0: 1, 2: 1}), (64, {3: 1, 5: 1})],
-    [(72, {0: 1, 1: 1}), (24, {1: 1, 2: 1, 3: 1, 4: 2})],
+    [(40, {3: 1, 4: 1}, 0), (56, {5: 2, 1: 1}, 1)],
+    [(56, {4: 1}, 0), (40, {5: 1, 0: 1}, 0), (48, {3: 2, 2: 1}, 1)],
+    [(40, {3: 1, 5: 1, 0: 1}, 0), (64, {4: 1}, 1)],
+    [(80, {1: 1, 2: 1}, 0), (56, {0: 1, 1: 1}, 1)],
+    [(64, {3: 1, 5: 1}, 0), (40, {0: 1, 2: 1}, 1)],
+    [(72, {0: 1, 1: 1}, 0), (40, {1: 1, 2: 1, 3: 1, 4: 1}, 1)],
 ]
 RET = [
-    [(72, {5: 1}, 0), (56, {3: 1}, 0), (40, {4: 1, 2: 1}, 1), (24, {1: 1}, 1)],
-    [(120, {3: 1}, 0), (96, {5: 1}, 1), (40, {0: 1}, 1)],
-    [(40, {3: 2, 1: 1}, 0), (32, {4: 1}, 1), (24, {5: 1}, 1)],
-    [(96, {1: 1}, 0), (32, {2: 1}, 0), (40, {0: 1, 4: 1}, 1), (24, {4: 1, 5: 1}, 1)],
-    [(64, {2: 1}, 0), (56, {1: 1}, 0), (40, {0: 1, 5: 1}, 1)],
-    [(112, {0: 1}, 0), (40, {1: 1, 2: 1}, 1), (64, {4: 1}, 1)],
+    [(24, {5: 3, 1: 1}, 0), (56, {3: 1}, 1), (40, {4: 1, 2: 1}, 1)],
+    [(80, {3: 1}, 0), (72, {5: 1}, 0), (40, {3: 1, 0: 1}, 1), (24, {5: 1}, 1)],
+    [(80, {3: 1}, 0), (32, {4: 1}, 1), (24, {5: 1}, 1), (40, {1: 1}, 1)],
+    [(40, {0: 1}, 0), (32, {2: 1, 4: 2}, 0), (96, {1: 1}, 1), (24, {5: 1}, 1)],
+    [(56, {1: 1}, 0), (40, {0: 1}, 0), (64, {2: 1}, 1), (40, {5: 1}, 1)],
+    [(40, {1: 1, 2: 1}, 0), (64, {4: 1}, 0), (112, {0: 1}, 1)],
 ]
-ORDER = [[5, 3, 4, 2, 1], [3, 5, 0], [3, 1, 4, 5], [1, 2, 0, 4, 5], [2, 1, 0, 5], [0, 1, 2, 4]]
-LMAX = 272
+LMAX = 352
 
 SCRATCH = {
+    "xp": ("sbuf", [128, NC], "float8_e4m3fn_x4"),
+    "xps": ("sbuf", [128, NC], "uint8"),
     "xt": ("sbuf", [128, 4 * NC], "bfloat16"),
     "w1t": ("sbuf", [128, 2048], "bfloat16"),
     "w2t": ("sbuf", [128, 512], "bfloat16"),
@@ -38,24 +41,24 @@ SCRATCH = {
     "s1s": ("sbuf", [128, 512], "uint8"),
     "s2q": ("sbuf", [128, 128], "float8_e4m3fn_x4"),
     "s2s": ("sbuf", [128, 128], "uint8"),
-    "ha": ("sbuf", [128, 4 * NC], "bfloat16"),
-    "hb": ("sbuf", [128, 4 * NC], "bfloat16"),
-    "haq": ("sbuf", [128, NC], "float8_e4m3fn_x4"),
-    "has": ("sbuf", [128, NC], "uint8"),
-    "hbq": ("sbuf", [128, NC], "float8_e4m3fn_x4"),
-    "hbs": ("sbuf", [128, NC], "uint8"),
+    "ha": ("sbuf", [128, 4 * LMAX], "bfloat16"),
+    "hb": ("sbuf", [128, 4 * LMAX], "bfloat16"),
+    "haq": ("sbuf", [128, LMAX], "float8_e4m3fn_x4"),
+    "has": ("sbuf", [128, LMAX], "uint8"),
+    "hbq": ("sbuf", [128, LMAX], "float8_e4m3fn_x4"),
+    "hbs": ("sbuf", [128, LMAX], "uint8"),
     "kt": ("sbuf", [128, 4 * NC], "bfloat16"),
     "kq": ("sbuf", [128, NC], "float8_e4m3fn_x4"),
     "ks": ("sbuf", [128, NC], "uint8"),
-    "p": ("sbuf", [128, LMAX + NC], "float32"),
+    "p": ("sbuf", [128, LMAX], "float32"),
     "land": ("sbuf", [128, NC], "float32"),
     "yt": ("sbuf", [128, NC], "float32"),
     "ps": ("psum", [128, 512 * 8], "float32"),
 }
-SEMAPHORES = (["ldx", "ldw1", "ldw2", "lds1", "lds2", "issued", "qx", "qw1", "qw2", "qs1", "qs2", "xin", "sent"]
+SEMAPHORES = (["ldp", "qp", "ldx", "ldw1", "ldw2", "lds1", "lds2", "issued", "qx", "qw1", "qw2", "qs1", "qs2", "xina", "xinb", "sent"]
               + ["z%d" % i for i in range(8)] + ["y%d" % i for i in range(4)]
               + ["ha4", "hb4", "k4", "qha", "qhb", "qk", "ppa", "ppb", "cpa", "cpb", "cpl", "u",
-                 "reton", "retoff", "addon", "addoff", "ston", "stoff"])
+                 "ret0", "ret1", "ret2", "add0", "add1", "add2", "st0", "st1", "st2"])
 
 
 def bits(mask):
@@ -89,43 +92,60 @@ def engines(src, dsts, topo):
 def make_plan(CNT, cores, topo):
     N = len(cores)
     off = [[sum(c[:e]) for e in range(N + 1)] for c in CNT]
-    base = [off[j][j] if CNT[j][j] else 0 for j in range(N)]
+    base = [off[j][j] if CNT[j][j] else BASE[j] for j in range(N)]
     rot = [[(off[j][e] - base[j]) % NC for e in range(N)] for j in range(N)]
-    total = {}
+    width = [{}, {}]
     for j in range(N):
-        for w, ds in SEND[j]:
+        for w, ds, part in SEND[j]:
             for e, k in ds.items():
-                total[j, e] = total.get((j, e), 0) + w * k
-    lw = [sum(total[j, e] for j in ORDER[e]) for e in range(N)]
-    L = [-(-w // 16) * 16 for w in lw]
-    first = [L[e] - lw[e] for e in range(N)]
-    n = [lw[e] + CNT[e][e] for e in range(N)]
-    mid = [n[e] - 128 for e in range(N)]
-    land, real, win = {}, {}, {}
+                width[part][j, e] = width[part].get((j, e), 0) + w * k
+    win, land, where, na, nb = {}, {}, {}, [0] * N, [0] * N
+    L = [0] * N
     for e in range(N):
-        p = first[e]
-        for j in ORDER[e]:
-            win[j, e] = min(rot[j][e], NC - total[j, e])
-            land[j, e] = p
-            real[j, e] = p - first[e] + rot[j][e] - win[j, e]
-            p += total[j, e]
-    sends, xin = [], [0] * N
+        nb[e] = sum(w for (j, f), w in width[1].items() if f == e)
+        na[e] = sum(w for (j, f), w in width[0].items() if f == e)
+        L[e] = -(-(na[e] + nb[e]) // 16) * 16
+        at = L[e] - na[e] - nb[e]
+        start = at
+        for part in (1, 0):
+            for j in range(N):
+                w = width[part].get((j, e), 0)
+                if not w:
+                    continue
+                every = width[0].get((j, e), 0) + width[1].get((j, e), 0)
+                x = min(rot[j][e], NC - every) + (width[0].get((j, e), 0) if part else 0)
+                win[part, j, e], land[part, j, e] = x, at
+                for c in range(w):
+                    if rot[j][e] <= x + c < rot[j][e] + CNT[j][e]:
+                        where[j, e, x + c - rot[j][e]] = (at + c - start, part)
+                at += w
+    first = [L[e] - na[e] - nb[e] for e in range(N)]
+    sends, xin = [], [[0] * N, [0] * N]
     for j in range(N):
-        done, calls = {}, []
-        for w, ds in SEND[j]:
+        calls, done = [], {}
+        for w, ds, part in SEND[j]:
             lst = [e for e, k in ds.items() for _ in range(k)]
             em = engines(cores[j], [cores[e] for e in lst], topo)
             tr = []
             for e in lst:
                 m, k = em[cores[e]].pop(0)
-                d = done.get(e, 0)
-                tr.append((e, win[j, e] + d, land[j, e] + d, m, k))
-                done[e] = d + w
-                xin[e] += 2 * k
-            calls.append((w, tr))
+                d = done.get((part, e), 0)
+                tr.append((e, win[part, j, e] + d, land[part, j, e] + d, m, k))
+                done[part, e] = d + w
+                xin[part][e] += 2 * k
+            calls.append((w, tr, part))
         sends.append(calls)
-    rets = []
-    ron, roff = [0] * N, [0] * N
+    early = []
+    for j in range(N):
+        ws = [(win[0, j, e], win[0, j, e] + w) for (i, e), w in width[0].items() if i == j]
+        a, b = min(w[0] for w in ws), max(w[1] for w in ws)
+        b = min(max(b, a + LEAST), NC)
+        early.append((min(a, b - LEAST), b))
+    for j in range(N):
+        sends[j] = [(w, [(e, s - (0 if part else early[j][0]), d, m, k) for e, s, d, m, k in tr], part)
+                    for w, tr, part in sends[j]]
+    rets, ret = [], [[0] * N, [0] * N, [0] * N]
+    kinds = [[1] * NC for _ in range(N)]
     for e in range(N):
         done, calls = {}, []
         for w, ds, part in RET[e]:
@@ -135,14 +155,15 @@ def make_plan(CNT, cores, topo):
             for j in lst:
                 m, k = em[cores[j]].pop(0)
                 d = done.get(j, 0)
-                p = real[j, e] + d
-                assert part or p + w <= mid[e], (e, j, p, w, mid[e])
-                tr.append((j, p, rot[j][e] + d, m, k))
+                cols = [where[j, e, d + c] for c in range(w)]
+                p = cols[0][0]
+                assert [c[0] for c in cols] == list(range(p, p + w)) and max(c[1] for c in cols) <= part, (e, j, w, part)
+                kind = 1 if topo.chip(cores[e]) == topo.chip(cores[j]) else 2 * part
+                tr.append((j, p, rot[j][e] + d, m, k, kind))
+                ret[kind][j] += k
+                for c in range(w):
+                    kinds[j][rot[j][e] + d + c] = kind
                 done[j] = d + w
-                if topo.chip(cores[e]) == topo.chip(cores[j]):
-                    ron[j] += k
-                else:
-                    roff[j] += k
             calls.append((w, tr, part))
         for j in range(N):
             assert done.get(j, 0) == (CNT[j][e] if j != e else 0), (e, j)
@@ -150,17 +171,13 @@ def make_plan(CNT, cores, topo):
     ranges = []
     for j in range(N):
         rs = []
-        for e in sorted(range(N), key=lambda e: rot[j][e]):
-            if not CNT[j][e]:
-                continue
-            far = topo.chip(cores[e]) != topo.chip(cores[j])
-            a = rot[j][e]
-            if rs and rs[-1][2] == far and off[j][e] != 0:
-                rs[-1][1] = a + CNT[j][e]
+        for c in range(NC):
+            if rs and rs[-1][2] == kinds[j][c] and (c + base[j]) % NC:
+                rs[-1][1] = c + 1
             else:
-                rs.append([a, a + CNT[j][e], far])
+                rs.append([c, c + 1, kinds[j][c]])
         ranges.append(rs)
-    return dict(L=L, first=first, n=n, mid=mid, base=base, sends=sends, xin=xin, rets=rets, ron=ron, roff=roff, ranges=ranges)
+    return dict(L=L, first=first, na=na, nb=nb, base=base, sends=sends, xin=xin, rets=rets, ret=ret, ranges=ranges, early=early)
 
 
 def rank_program(g, core, T, topo):
@@ -171,10 +188,11 @@ def rank_program(g, core, T, topo):
     cores = T.cores
     P = make_plan(CNT, cores, topo)
     S = T.sem
-    L, first, n, mid, base = P["L"][rank], P["first"][rank], P["n"][rank], P["mid"][rank], P["base"][rank]
+    L, first, na, nb, base = P["L"][rank], P["first"][rank], P["na"][rank], P["nb"][rank], P["base"][rank]
     own = CNT[rank][rank]
     U8 = dt.uint8
-    sizes = (mid, n - mid)
+    sizes = (na + own, max(nb, LEAST))
+    starts = (first + nb, first)
 
     def bank(k, w):
         return T.ps[:, 512 * k:512 * k + w]
@@ -190,23 +208,28 @@ def rank_program(g, core, T, topo):
                             for i, (c, d, s, m, k) in enumerate(trs)], local_sem=S.sent)
         sent[0] += sum(t[4] for t in trs)
 
+    ea, eb = P["early"][rank]
     cut = NC - base
-    g.sync.dma_start(T.xt[:, 0:4 * cut], T.x[:, 4 * base:4 * NC]).then_inc(S.ldx, 16)
-    if base:
-        g.scalar.dma_start(T.xt[:, 4 * cut:4 * NC], T.x[:, 0:4 * base]).then_inc(S.ldx, 16)
+    waits = []
+    for sem, runs in ((S.ldp, ((ea, eb),)), (S.ldx, ((0, ea), (eb, NC)))):
+        pieces = [(max(a, lo), min(b, hi), x0) for a, b in runs for lo, hi, x0 in ((0, cut, base), (cut, NC, -cut))]
+        pieces = [(a, b, x0) for a, b, x0 in pieces if a < b]
+        for i, (a, b, x0) in enumerate(pieces):
+            (g.scalar if i % 2 else g.sync).dma_start(T.xt[:, 4 * a:4 * b], T.x[:, 4 * (a + x0):4 * (b + x0)]).then_inc(sem, 16)
+        waits.append(16 * len(pieces))
     g.sync.dma_start(T.w1t[:], T.w1[:]).then_inc(S.ldw1, 16)
     g.sync.dma_start(T.w2t[:], T.w2[:]).then_inc(S.ldw2, 16)
-    g.sync.wait_ge(S.issued, 1)
     g.sync.dma_start(T.s1t[:], T.s1[:]).then_inc(S.lds1, 16)
+    g.sync.wait_ge(S.issued, 1)
     g.sync.dma_start(T.s2t[:], T.s2[:]).then_inc(S.lds2, 16)
 
-    g.wait_ge(S.qx, 1)
-    for w, tr in P["sends"][rank]:
-        fused([(cores[e], T.xq[:, d:d + w].bitcast(U8), T.xq[:, L + s:L + s + w].bitcast(U8), m, k) for e, s, d, m, k in tr],
-              [S.xin] * len(tr))
-    for w, tr in P["sends"][rank]:
-        fused([(cores[e], T.xs[:, d:d + w], T.xs[:, L + s:L + s + w], m, k) for e, s, d, m, k in tr],
-              [S.xin] * len(tr))
+    for part, q, s_, o in ((0, T.xp, T.xps, 0), (1, T.xq, T.xs, L)):
+        g.wait_ge(S.qx if part else S.qp, 1)
+        calls = [(w, tr, [S.xinb if part else S.xina] * len(tr)) for w, tr, f in P["sends"][rank] if f == part]
+        for w, tr, sem in calls:
+            fused([(cores[e], T.xq[:, d:d + w].bitcast(U8), q[:, o + s:o + s + w].bitcast(U8), m, k) for e, s, d, m, k in tr], sem)
+        for w, tr, sem in calls:
+            fused([(cores[e], T.xs[:, d:d + w], s_[:, o + s:o + s + w], m, k) for e, s, d, m, k in tr], sem)
     g.sem_inc(S.issued, 1)
     have = 0
     for w, tr, part in P["rets"][rank]:
@@ -214,26 +237,32 @@ def rank_program(g, core, T, topo):
             for sem in (S.cpa, S.cpb)[have:part + 1]:
                 g.wait_ge(sem, 1)
             have = part + 1
-        fused([(cores[j], T.land[:, d:d + w], T.p[:, s:s + w], m, k) for j, s, d, m, k in tr],
-              [S.reton if topo.chip(cores[j]) == topo.chip(core) else S.retoff for j, s, d, m, k in tr])
+        fused([(cores[j], T.land[:, d:d + w], T.p[:, s:s + w], m, k) for j, s, d, m, k, f in tr],
+              [S["ret%d" % f] for j, s, d, m, k, f in tr])
     g.wait_ge(S.sent, sent[0])
 
     t = g.tensor
-    t.wait_ge(S.qw1, 1)
-    t.wait_ge(S.qx, 1)
-    t.wait_ge(S.xin, P["xin"][rank])
-    for part in (0, 1):
-        a = first + (mid if part else 0)
-        b = a + sizes[part]
+
+    def up(part):
+        a, w = starts[part], sizes[part]
+        t.wait_ge(S.xinb if part else S.xina, P["xin"][part][rank])
         for i in range(4):
-            t.matmul_mx(bank(4 * part + i, sizes[part]), T.w1q[:, 128 * i:128 * i + 128], T.w1s[:, 128 * i:128 * i + 128],
-                        T.xq[:, a:b], T.xs[:, a:b], True, True).then_inc(S["z%d" % (4 * part + i)], 1)
-    t.wait_ge(S.qw2, 1)
-    for part in (0, 1):
+            t.matmul_mx(bank(4 * part + i, w), T.w1q[:, 128 * i:128 * i + 128], T.w1s[:, 128 * i:128 * i + 128],
+                        T.xq[:, a:a + w], T.xs[:, a:a + w], True, True).then_inc(S["z%d" % (4 * part + i)], 1)
+
+    def down(part):
         t.wait_ge(S["qhb"] if part else S["qha"], 1)
         q, s = (T.hbq, T.hbs) if part else (T.haq, T.has)
         t.matmul_mx(bank(4 * part, sizes[part]), T.w2q[:], T.w2s[:], q[:, 0:sizes[part]], s[:, 0:sizes[part]],
                     True, True).then_inc(S["ppb"] if part else S["ppa"], 1)
+
+    t.wait_ge(S.qw1, 1)
+    t.wait_ge(S.qx, 1)
+    up(0)
+    t.wait_ge(S.qw2, 1)
+    down(0)
+    up(1)
+    down(1)
     YB = (1, 2, 3, 5)
     t.wait_ge(S.qs1, 1)
     for i in range(4):
@@ -251,13 +280,7 @@ def rank_program(g, core, T, topo):
     def step_s(out, in_, sem):
         sc.activation(out, in_, ActivationFunctionType.Relu, scale=C).then_inc(sem, 1)
 
-    v.wait_ge(S.ldx, 32 if base else 16)
-    v.quantize_mx(T.xq[:, L:L + NC], T.xs[:, L:L + NC], T.xt[:]).then_inc(S.qx, 1)
-    v.wait_ge(S.ldw1, 16)
-    v.quantize_mx(T.w1q[:], T.w1s[:], T.w1t[:]).then_inc(S.qw1, 1)
-    v.wait_ge(S.ldw2, 16)
-    v.quantize_mx(T.w2q[:], T.w2s[:], T.w2t[:]).then_inc(S.qw2, 1)
-    for part in (0, 1):
+    def steps(part):
         w = sizes[part]
         h, q, s = (T.hb, T.hbq, T.hbs) if part else (T.ha, T.haq, T.has)
         done = S["hb4"] if part else S["ha4"]
@@ -269,15 +292,27 @@ def rank_program(g, core, T, topo):
             step_v(h[:, i:4 * w:4], bank(4 * part + i, w), done)
         v.wait_ge(done, 4)
         v.quantize_mx(q[:, 0:w], s[:, 0:w], h[:, 0:4 * w]).then_inc(S["qhb"] if part else S["qha"], 1)
-    sc.wait_ge(S.ppa, 1)
-    sc.activation(T.p[:, 0:mid], bank(0, mid), ActivationFunctionType.Copy).then_inc(S.cpa, 1)
-    v.wait_ge(S.ppb, 1)
-    wb = sizes[1]
-    v.tensor_copy(T.p[:, mid:n - own], bank(4, wb - own)).then_inc(S.cpb, 1)
-    if own:
-        v.tensor_copy(T.land[:, 0:own], T.ps[:, 512 * 4 + wb - own:512 * 4 + wb]).then_inc(S.cpl, 1)
+
+    v.wait_ge(S.ldp, waits[0])
+    v.quantize_mx(T.xp[:, 0:eb - ea], T.xps[:, 0:eb - ea], T.xt[:, 4 * ea:4 * eb]).then_inc(S.qp, 1)
+    if waits[1]:
+        v.wait_ge(S.ldx, waits[1])
+    v.quantize_mx(T.xq[:, L:L + NC], T.xs[:, L:L + NC], T.xt[:]).then_inc(S.qx, 1)
+    v.wait_ge(S.ldw1, 16)
+    v.quantize_mx(T.w1q[:], T.w1s[:], T.w1t[:]).then_inc(S.qw1, 1)
+    v.wait_ge(S.ldw2, 16)
+    v.quantize_mx(T.w2q[:], T.w2s[:], T.w2t[:]).then_inc(S.qw2, 1)
     v.wait_ge(S.lds1, 16)
     v.quantize_mx(T.s1q[:], T.s1s[:], T.s1t[:]).then_inc(S.qs1, 1)
+    steps(0)
+    sc.wait_ge(S.ppa, 1)
+    sc.activation(T.p[:, nb:nb + na], bank(0, na), ActivationFunctionType.Copy).then_inc(S.cpa, 1)
+    steps(1)
+    sc.wait_ge(S.ppb, 1)
+    sc.activation(T.p[:, 0:nb], bank(4, nb), ActivationFunctionType.Copy).then_inc(S.cpb, 1)
+    if own:
+        v.wait_ge(S.cpa, 1)
+        v.tensor_copy(T.land[:, 0:own], T.ps[:, na:na + own]).then_inc(S.cpl, 1)
     v.wait_ge(S.lds2, 16)
     v.quantize_mx(T.s2q[:], T.s2s[:], T.s2t[:]).then_inc(S.qs2, 1)
     for i in (0, 2):
@@ -292,17 +327,19 @@ def rank_program(g, core, T, topo):
     v.wait_ge(S.u, 1)
     if own:
         v.wait_ge(S.cpl, 1)
-    for far, ret, add, st, q in ((False, "reton", "addon", "ston", sc), (True, "retoff", "addoff", "stoff", g.sync)):
-        rs = [r for r in P["ranges"][rank] if r[2] == far]
+    wait = []
+    for kind, q in ((0, sc), (1, sc), (2, g.sync)):
+        rs = [r for r in P["ranges"][rank] if r[2] == kind]
         if not rs:
             continue
-        count = P["roff" if far else "ron"][rank]
-        if count:
-            v.wait_ge(S[ret], count)
+        if P["ret"][kind][rank]:
+            v.wait_ge(S["ret%d" % kind], P["ret"][kind][rank])
         for a, b, _ in rs:
-            v.tensor_tensor(T.yt[:, a:b], T.ps[:, 512 * 6 + a:512 * 6 + b], T.land[:, a:b], AluOpType.add).then_inc(S[add], 1)
-        q.wait_ge(S[add], len(rs))
+            v.tensor_tensor(T.yt[:, a:b], T.ps[:, 512 * 6 + a:512 * 6 + b], T.land[:, a:b], AluOpType.add).then_inc(S["add%d" % kind], 1)
+        q.wait_ge(S["add%d" % kind], len(rs))
         for a, b, _ in rs:
             c = (a + base) % NC
-            q.dma_start(T.y[:, c:c + b - a], T.yt[:, a:b]).then_inc(S[st], 16)
-        q.wait_ge(S[st], 16 * len(rs))
+            q.dma_start(T.y[:, c:c + b - a], T.yt[:, a:b]).then_inc(S["st%d" % kind], 16)
+        wait.append((q, kind, 16 * len(rs)))
+    for q, kind, k in wait:
+        q.wait_ge(S["st%d" % kind], k)

from concourse.bass import DstId, RemoteDMATransfer
from concourse.mybir import dt, AluOpType, ActivationFunctionType

C = 0.023
NC = 256
LEAST = 128
BASE = [0, 160, 0, 0, 0, 0]
SEND = [
    [(40, {3: 1, 4: 1}, 0), (56, {5: 2, 1: 1}, 1)],
    [(56, {4: 1}, 0), (40, {5: 1, 0: 1}, 0), (48, {3: 2, 2: 1}, 1)],
    [(40, {3: 1, 5: 1, 0: 1}, 0), (64, {4: 1}, 1)],
    [(80, {1: 1, 2: 1}, 0), (56, {0: 1, 1: 1}, 1)],
    [(64, {3: 1, 5: 1}, 0), (40, {0: 1, 2: 1}, 1)],
    [(72, {0: 1, 1: 1}, 0), (40, {1: 1, 2: 1, 3: 1, 4: 1}, 1)],
]
RET = [
    [(24, {5: 3, 1: 1}, 0), (56, {3: 1}, 1), (40, {4: 1, 2: 1}, 1)],
    [(80, {3: 1}, 0), (72, {5: 1}, 0), (40, {3: 1, 0: 1}, 1), (24, {5: 1}, 1)],
    [(80, {3: 1}, 0), (32, {4: 1}, 1), (24, {5: 1}, 1), (40, {1: 1}, 1)],
    [(40, {0: 1}, 0), (32, {2: 1, 4: 2}, 0), (96, {1: 1}, 1), (24, {5: 1}, 1)],
    [(56, {1: 1}, 0), (40, {0: 1}, 0), (64, {2: 1}, 1), (40, {5: 1}, 1)],
    [(40, {1: 1, 2: 1}, 0), (64, {4: 1}, 0), (112, {0: 1}, 1)],
]
LMAX = 352

SCRATCH = {
    "xp": ("sbuf", [128, NC], "float8_e4m3fn_x4"),
    "xps": ("sbuf", [128, NC], "uint8"),
    "xt": ("sbuf", [128, 4 * NC], "bfloat16"),
    "w1t": ("sbuf", [128, 2048], "bfloat16"),
    "w2t": ("sbuf", [128, 512], "bfloat16"),
    "s1t": ("sbuf", [128, 2048], "bfloat16"),
    "s2t": ("sbuf", [128, 512], "bfloat16"),
    "xq": ("sbuf", [128, LMAX + NC], "float8_e4m3fn_x4"),
    "xs": ("sbuf", [128, LMAX + NC], "uint8"),
    "w1q": ("sbuf", [128, 512], "float8_e4m3fn_x4"),
    "w1s": ("sbuf", [128, 512], "uint8"),
    "w2q": ("sbuf", [128, 128], "float8_e4m3fn_x4"),
    "w2s": ("sbuf", [128, 128], "uint8"),
    "s1q": ("sbuf", [128, 512], "float8_e4m3fn_x4"),
    "s1s": ("sbuf", [128, 512], "uint8"),
    "s2q": ("sbuf", [128, 128], "float8_e4m3fn_x4"),
    "s2s": ("sbuf", [128, 128], "uint8"),
    "ha": ("sbuf", [128, 4 * LMAX], "bfloat16"),
    "hb": ("sbuf", [128, 4 * LMAX], "bfloat16"),
    "haq": ("sbuf", [128, LMAX], "float8_e4m3fn_x4"),
    "has": ("sbuf", [128, LMAX], "uint8"),
    "hbq": ("sbuf", [128, LMAX], "float8_e4m3fn_x4"),
    "hbs": ("sbuf", [128, LMAX], "uint8"),
    "kt": ("sbuf", [128, 4 * NC], "bfloat16"),
    "kq": ("sbuf", [128, NC], "float8_e4m3fn_x4"),
    "ks": ("sbuf", [128, NC], "uint8"),
    "p": ("sbuf", [128, LMAX], "float32"),
    "land": ("sbuf", [128, NC], "float32"),
    "yt": ("sbuf", [128, NC], "float32"),
    "ps": ("psum", [128, 512 * 8], "float32"),
}
SEMAPHORES = (["ldp", "qp", "ldx", "ldw1", "ldw2", "lds1", "lds2", "issued", "qx", "qw1", "qw2", "qs1", "qs2", "xina", "xinb", "sent"]
              + ["z%d" % i for i in range(8)] + ["y%d" % i for i in range(4)]
              + ["ha4", "hb4", "k4", "qha", "qhb", "qk", "ppa", "ppb", "cpa", "cpb", "cpl", "u",
                 "ret0", "ret1", "ret2", "add0", "add1", "add2", "st0", "st1", "st2"])


def bits(mask):
    return [i for i in range(16) if mask >> i & 1]


def engines(src, dsts, topo):
    far = [d for d in dsts if topo.chip(d) != topo.chip(src)]
    near = [d for d in dsts if topo.chip(d) == topo.chip(src)]
    out, taken = {}, 0
    for group in (far, near):
        if not group:
            continue
        free = bits(topo.mask(src, group[0]) & ~taken)
        base = 1
        while base * 2 * len(group) <= len(free):
            base *= 2
        size = [base] * len(group)
        for i in range(len(group)):
            if sum(size) + size[i] <= len(free):
                size[i] *= 2
        at = 0
        for i, d in enumerate(group):
            m = sum(1 << b for b in free[at:at + size[i]])
            at += size[i]
            out.setdefault(d, []).append((m, size[i]))
        taken |= topo.mask(src, group[0])
    return out


def make_plan(CNT, cores, topo):
    N = len(cores)
    off = [[sum(c[:e]) for e in range(N + 1)] for c in CNT]
    base = [off[j][j] if CNT[j][j] else BASE[j] for j in range(N)]
    rot = [[(off[j][e] - base[j]) % NC for e in range(N)] for j in range(N)]
    width = [{}, {}]
    for j in range(N):
        for w, ds, part in SEND[j]:
            for e, k in ds.items():
                width[part][j, e] = width[part].get((j, e), 0) + w * k
    win, land, where, na, nb = {}, {}, {}, [0] * N, [0] * N
    L = [0] * N
    for e in range(N):
        nb[e] = sum(w for (j, f), w in width[1].items() if f == e)
        na[e] = sum(w for (j, f), w in width[0].items() if f == e)
        L[e] = -(-(na[e] + nb[e]) // 16) * 16
        at = L[e] - na[e] - nb[e]
        start = at
        for part in (1, 0):
            for j in range(N):
                w = width[part].get((j, e), 0)
                if not w:
                    continue
                every = width[0].get((j, e), 0) + width[1].get((j, e), 0)
                x = min(rot[j][e], NC - every) + (width[0].get((j, e), 0) if part else 0)
                win[part, j, e], land[part, j, e] = x, at
                for c in range(w):
                    if rot[j][e] <= x + c < rot[j][e] + CNT[j][e]:
                        where[j, e, x + c - rot[j][e]] = (at + c - start, part)
                at += w
    first = [L[e] - na[e] - nb[e] for e in range(N)]
    sends, xin = [], [[0] * N, [0] * N]
    for j in range(N):
        calls, done = [], {}
        for w, ds, part in SEND[j]:
            lst = [e for e, k in ds.items() for _ in range(k)]
            em = engines(cores[j], [cores[e] for e in lst], topo)
            tr = []
            for e in lst:
                m, k = em[cores[e]].pop(0)
                d = done.get((part, e), 0)
                tr.append((e, win[part, j, e] + d, land[part, j, e] + d, m, k))
                done[part, e] = d + w
                xin[part][e] += 2 * k
            calls.append((w, tr, part))
        sends.append(calls)
    early = []
    for j in range(N):
        ws = [(win[0, j, e], win[0, j, e] + w) for (i, e), w in width[0].items() if i == j]
        a, b = min(w[0] for w in ws), max(w[1] for w in ws)
        b = min(max(b, a + LEAST), NC)
        early.append((min(a, b - LEAST), b))
    for j in range(N):
        sends[j] = [(w, [(e, s - (0 if part else early[j][0]), d, m, k) for e, s, d, m, k in tr], part)
                    for w, tr, part in sends[j]]
    rets, ret = [], [[0] * N, [0] * N, [0] * N]
    kinds = [[1] * NC for _ in range(N)]
    for e in range(N):
        done, calls = {}, []
        for w, ds, part in RET[e]:
            lst = [j for j, k in ds.items() for _ in range(k)]
            em = engines(cores[e], [cores[j] for j in lst], topo)
            tr = []
            for j in lst:
                m, k = em[cores[j]].pop(0)
                d = done.get(j, 0)
                cols = [where[j, e, d + c] for c in range(w)]
                p = cols[0][0]
                assert [c[0] for c in cols] == list(range(p, p + w)) and max(c[1] for c in cols) <= part, (e, j, w, part)
                kind = 1 if topo.chip(cores[e]) == topo.chip(cores[j]) else 2 * part
                tr.append((j, p, rot[j][e] + d, m, k, kind))
                ret[kind][j] += k
                for c in range(w):
                    kinds[j][rot[j][e] + d + c] = kind
                done[j] = d + w
            calls.append((w, tr, part))
        for j in range(N):
            assert done.get(j, 0) == (CNT[j][e] if j != e else 0), (e, j)
        rets.append(calls)
    ranges = []
    for j in range(N):
        rs = []
        for c in range(NC):
            if rs and rs[-1][2] == kinds[j][c] and (c + base[j]) % NC:
                rs[-1][1] = c + 1
            else:
                rs.append([c, c + 1, kinds[j][c]])
        ranges.append(rs)
    return dict(L=L, first=first, na=na, nb=nb, base=base, sends=sends, xin=xin, rets=rets, ret=ret, ranges=ranges, early=early)


def rank_program(g, core, T, topo):
    rank = T.rank_of(core)
    if rank is None:
        return
    CNT = T.tables["CNT"]
    cores = T.cores
    P = make_plan(CNT, cores, topo)
    S = T.sem
    L, first, na, nb, base = P["L"][rank], P["first"][rank], P["na"][rank], P["nb"][rank], P["base"][rank]
    own = CNT[rank][rank]
    U8 = dt.uint8
    sizes = (na + own, max(nb, LEAST))
    starts = (first + nb, first)

    def bank(k, w):
        return T.ps[:, 512 * k:512 * k + w]

    def dst(c):
        rid, pid, _ = topo.addr(c)
        return DstId(rid=rid, pnc=pid)

    sent = [0]

    def fused(trs, sem):
        g.remote_dma_fused([RemoteDMATransfer(dst_ids=[dst(c)], dma_engine_mask=m, remote_sem=sem[i], srcs=[s], dsts=[d])
                            for i, (c, d, s, m, k) in enumerate(trs)], local_sem=S.sent)
        sent[0] += sum(t[4] for t in trs)

    ea, eb = P["early"][rank]
    cut = NC - base
    waits = []
    for sem, runs in ((S.ldp, ((ea, eb),)), (S.ldx, ((0, ea), (eb, NC)))):
        pieces = [(max(a, lo), min(b, hi), x0) for a, b in runs for lo, hi, x0 in ((0, cut, base), (cut, NC, -cut))]
        pieces = [(a, b, x0) for a, b, x0 in pieces if a < b]
        for i, (a, b, x0) in enumerate(pieces):
            (g.scalar if i % 2 else g.sync).dma_start(T.xt[:, 4 * a:4 * b], T.x[:, 4 * (a + x0):4 * (b + x0)]).then_inc(sem, 16)
        waits.append(16 * len(pieces))
    g.sync.dma_start(T.w1t[:], T.w1[:]).then_inc(S.ldw1, 16)
    g.sync.dma_start(T.w2t[:], T.w2[:]).then_inc(S.ldw2, 16)
    g.sync.dma_start(T.s1t[:], T.s1[:]).then_inc(S.lds1, 16)
    g.sync.wait_ge(S.issued, 1)
    g.sync.dma_start(T.s2t[:], T.s2[:]).then_inc(S.lds2, 16)

    for part, q, s_, o in ((0, T.xp, T.xps, 0), (1, T.xq, T.xs, L)):
        g.wait_ge(S.qx if part else S.qp, 1)
        calls = [(w, tr, [S.xinb if part else S.xina] * len(tr)) for w, tr, f in P["sends"][rank] if f == part]
        for w, tr, sem in calls:
            fused([(cores[e], T.xq[:, d:d + w].bitcast(U8), q[:, o + s:o + s + w].bitcast(U8), m, k) for e, s, d, m, k in tr], sem)
        for w, tr, sem in calls:
            fused([(cores[e], T.xs[:, d:d + w], s_[:, o + s:o + s + w], m, k) for e, s, d, m, k in tr], sem)
    g.sem_inc(S.issued, 1)
    have = 0
    for w, tr, part in P["rets"][rank]:
        if have <= part:
            for sem in (S.cpa, S.cpb)[have:part + 1]:
                g.wait_ge(sem, 1)
            have = part + 1
        fused([(cores[j], T.land[:, d:d + w], T.p[:, s:s + w], m, k) for j, s, d, m, k, f in tr],
              [S["ret%d" % f] for j, s, d, m, k, f in tr])
    g.wait_ge(S.sent, sent[0])

    t = g.tensor

    def up(part):
        a, w = starts[part], sizes[part]
        t.wait_ge(S.xinb if part else S.xina, P["xin"][part][rank])
        for i in range(4):
            t.matmul_mx(bank(4 * part + i, w), T.w1q[:, 128 * i:128 * i + 128], T.w1s[:, 128 * i:128 * i + 128],
                        T.xq[:, a:a + w], T.xs[:, a:a + w], True, True).then_inc(S["z%d" % (4 * part + i)], 1)

    def down(part):
        t.wait_ge(S["qhb"] if part else S["qha"], 1)
        q, s = (T.hbq, T.hbs) if part else (T.haq, T.has)
        t.matmul_mx(bank(4 * part, sizes[part]), T.w2q[:], T.w2s[:], q[:, 0:sizes[part]], s[:, 0:sizes[part]],
                    True, True).then_inc(S["ppb"] if part else S["ppa"], 1)

    t.wait_ge(S.qw1, 1)
    t.wait_ge(S.qx, 1)
    up(0)
    t.wait_ge(S.qw2, 1)
    down(0)
    up(1)
    down(1)
    YB = (1, 2, 3, 5)
    t.wait_ge(S.qs1, 1)
    for i in range(4):
        t.matmul_mx(bank(YB[i], NC), T.s1q[:, 128 * i:128 * i + 128], T.s1s[:, 128 * i:128 * i + 128],
                    T.xq[:, L:L + NC], T.xs[:, L:L + NC], True, True).then_inc(S["y%d" % i], 1)
    t.wait_ge(S.qs2, 1)
    t.wait_ge(S.qk, 1)
    t.matmul_mx(bank(6, NC), T.s2q[:], T.s2s[:], T.kq[:], T.ks[:], True, True).then_inc(S.u, 1)

    v, sc = g.vector, g.scalar

    def step_v(out, in_, sem):
        v.tensor_scalar(out, in_, 0.0, C, AluOpType.max, AluOpType.mult).then_inc(sem, 1)

    def step_s(out, in_, sem):
        sc.activation(out, in_, ActivationFunctionType.Relu, scale=C).then_inc(sem, 1)

    def steps(part):
        w = sizes[part]
        h, q, s = (T.hb, T.hbq, T.hbs) if part else (T.ha, T.haq, T.has)
        done = S["hb4"] if part else S["ha4"]
        for i in (0, 2):
            sc.wait_ge(S["z%d" % (4 * part + i)], 1)
            step_s(h[:, i:4 * w:4], bank(4 * part + i, w), done)
        for i in (1, 3):
            v.wait_ge(S["z%d" % (4 * part + i)], 1)
            step_v(h[:, i:4 * w:4], bank(4 * part + i, w), done)
        v.wait_ge(done, 4)
        v.quantize_mx(q[:, 0:w], s[:, 0:w], h[:, 0:4 * w]).then_inc(S["qhb"] if part else S["qha"], 1)

    v.wait_ge(S.ldp, waits[0])
    v.quantize_mx(T.xp[:, 0:eb - ea], T.xps[:, 0:eb - ea], T.xt[:, 4 * ea:4 * eb]).then_inc(S.qp, 1)
    if waits[1]:
        v.wait_ge(S.ldx, waits[1])
    v.quantize_mx(T.xq[:, L:L + NC], T.xs[:, L:L + NC], T.xt[:]).then_inc(S.qx, 1)
    v.wait_ge(S.ldw1, 16)
    v.quantize_mx(T.w1q[:], T.w1s[:], T.w1t[:]).then_inc(S.qw1, 1)
    v.wait_ge(S.ldw2, 16)
    v.quantize_mx(T.w2q[:], T.w2s[:], T.w2t[:]).then_inc(S.qw2, 1)
    v.wait_ge(S.lds1, 16)
    v.quantize_mx(T.s1q[:], T.s1s[:], T.s1t[:]).then_inc(S.qs1, 1)
    steps(0)
    sc.wait_ge(S.ppa, 1)
    sc.activation(T.p[:, nb:nb + na], bank(0, na), ActivationFunctionType.Copy).then_inc(S.cpa, 1)
    steps(1)
    sc.wait_ge(S.ppb, 1)
    sc.activation(T.p[:, 0:nb], bank(4, nb), ActivationFunctionType.Copy).then_inc(S.cpb, 1)
    if own:
        v.wait_ge(S.cpa, 1)
        v.tensor_copy(T.land[:, 0:own], T.ps[:, na:na + own]).then_inc(S.cpl, 1)
    v.wait_ge(S.lds2, 16)
    v.quantize_mx(T.s2q[:], T.s2s[:], T.s2t[:]).then_inc(S.qs2, 1)
    for i in (0, 2):
        sc.wait_ge(S["y%d" % i], 1)
        step_s(T.kt[:, i:4 * NC:4], bank(YB[i], NC), S.k4)
    for i in (1, 3):
        v.wait_ge(S["y%d" % i], 1)
        step_v(T.kt[:, i:4 * NC:4], bank(YB[i], NC), S.k4)
    v.wait_ge(S.k4, 4)
    v.quantize_mx(T.kq[:], T.ks[:], T.kt[:]).then_inc(S.qk, 1)

    v.wait_ge(S.u, 1)
    if own:
        v.wait_ge(S.cpl, 1)
    wait = []
    for kind, q in ((0, sc), (1, sc), (2, g.sync)):
        rs = [r for r in P["ranges"][rank] if r[2] == kind]
        if not rs:
            continue
        if P["ret"][kind][rank]:
            v.wait_ge(S["ret%d" % kind], P["ret"][kind][rank])
        for a, b, _ in rs:
            v.tensor_tensor(T.yt[:, a:b], T.ps[:, 512 * 6 + a:512 * 6 + b], T.land[:, a:b], AluOpType.add).then_inc(S["add%d" % kind], 1)
        q.wait_ge(S["add%d" % kind], len(rs))
        for a, b, _ in rs:
            c = (a + base) % NC
            q.dma_start(T.y[:, c:c + b - a], T.yt[:, a:b]).then_inc(S["st%d" % kind], 16)
        wait.append((q, kind, 16 * len(rs)))
    for q, kind, k in wait:
        q.wait_ge(S["st%d" % kind], k)
